import numpy as np
import ml_dtypes


def mxq(x, axis, fmt="e4m3"):
    dtype, down = {"e4m3": (ml_dtypes.float8_e4m3fn, 7), "e5m2": (ml_dtypes.float8_e5m2, 14)}[fmt]
    v = np.moveaxis(np.asarray(x, np.float32).astype(ml_dtypes.bfloat16).astype(np.float64), axis, -1)
    blocks = v.reshape(v.shape[:-1] + (-1, 32))
    amax = np.abs(blocks).max(-1, keepdims=True)
    byte = np.maximum(np.where(amax > 0, np.frexp(amax)[1] - 1 + 127, 0) - down, 1)
    scale = np.exp2(byte - 127.0)
    codes = (blocks / scale).astype(np.float32).astype(dtype).astype(np.float64)
    return np.moveaxis((codes * scale).reshape(v.shape), -1, axis)


WIDE = False


def mx_kscale(k):
    if not WIDE:
        return np.ones(k)
    levels = np.array([10, -10, 5, -5, 0])
    if k % 512:
        return np.exp2(np.random.permutation(np.resize(levels, k // 32))).repeat(32)
    a = np.empty((k // 512, 16))
    for p in range(k // 512):
        a[p, :8] = np.random.permutation(np.resize(levels, 8))
        for g in range(8):
            far = levels[np.abs(levels - a[p, g]) >= 10]
            a[p, g + 8] = far[np.random.randint(len(far))]
    return np.exp2(a.ravel()).repeat(32)


def f64(x):
    return np.asarray(x).astype(np.float64)


def striped8(idx):
    return np.asarray(idx).reshape(8, -1, 16).transpose(0, 2, 1).reshape(128, -1).astype(np.uint16)


def unstriped8(offs):
    return offs.reshape(8, 16, -1).transpose(0, 2, 1).reshape(8, -1).astype(np.int64)


def pick8(x, idx, run):
    r = np.arange(len(x))
    return x[r[:, None], idx[r % (8 * run) // run]]


E2M1 = np.array([0.0, 0.5, 1.0, 1.5, 2.0, 3.0, 4.0, 6.0, -0.0, -0.5, -1.0, -1.5, -2.0, -3.0, -4.0, -6.0])


def pack_weight(w, fmt):
    k, n = w.shape
    w = f64(np.asarray(w, np.float32).astype(ml_dtypes.bfloat16)).reshape(k // 32, 32, n)
    amax = np.abs(w).max(1)
    if fmt == "e4m3":
        byte = np.frexp(amax)[1] - 1 + 127 - 7
    else:
        mant, ex = np.frexp(amax / 6.0)
        byte = np.where(mant > 0.5, ex, ex - 1) + 127
    byte = np.clip(np.where(amax > 0, byte, 1), 1, 254)
    scaled = (w * np.exp2(127.0 - byte)[:, None, :]).reshape(k, n).astype(np.float32)
    by_word = np.ascontiguousarray(scaled.reshape(k // 512, 128, 4, n).transpose(0, 1, 3, 2))
    if fmt == "e4m3":
        words = by_word.astype(ml_dtypes.float8_e4m3fn).view(np.uint8)
    else:
        c = by_word.astype(ml_dtypes.float4_e2m1fn).view(np.uint8) & 0xF
        words = (c[..., 0::2] | (c[..., 1::2] << 4)).reshape(k // 512, 128, 2 * n)
    return np.ascontiguousarray(words), np.ascontiguousarray(byte.astype(np.uint8).reshape(k // 512, 16, n))


def unpack_weight(words, scales, fmt):
    g, _, n = scales.shape
    words = np.ascontiguousarray(words).reshape(g, 128, n, -1)
    if fmt == "e4m3":
        vals = words.view(ml_dtypes.float8_e4m3fn).astype(np.float64)
    else:
        nib = np.empty((g, 128, n, 4), np.uint8)
        nib[..., 0::2] = words & 0xF
        nib[..., 1::2] = words >> 4
        vals = E2M1[nib]
    vals = vals * np.repeat(np.exp2(scales.astype(np.float64) - 127.0), 8, axis=1)[..., None]
    return vals.transpose(0, 1, 3, 2).reshape(g * 512, n)


D, T, U, X, I, Q = 512, 1024, 1024, 1024, 512, 128


def setup_inputs():
    n = np.random.standard_normal
    idx = np.stack([np.random.permutation(T)[:I] for _ in range(8)])
    idx2 = np.stack([np.random.permutation(U)[:I] for _ in range(8)])
    idx3 = np.stack([np.random.permutation(X)[:I] for _ in range(8)])
    idx4 = np.stack([np.random.permutation(X)[:I] for _ in range(8)])
    idx5 = np.stack([np.random.permutation(T)[:I] for _ in range(8)])
    idx6 = np.stack([np.random.permutation(T)[:I] for _ in range(8)])
    fd = mx_kscale(D)
    keysp = pack_weight(n((D, T)) / fd[:, None], "e2m1")
    notesp = pack_weight(n((D, U)) / fd[:, None], "e4m3")
    usersp = pack_weight(n((D, X)) / fd[:, None], "e2m1")
    return {
        "query": (n((D, Q)) * 1.0 / np.sqrt(D) * fd[:, None]).astype(np.float32),
        "keys_words": keysp[0],
        "keys_scales": keysp[1],
        "notes_words": notesp[0],
        "notes_scales": notesp[1],
        "users_words": usersp[0],
        "users_scales": usersp[1],
        "offs": striped8(idx),
        "offs2": striped8(idx2),
        "offs3": striped8(idx3),
        "offs4": striped8(idx4),
        "offs5": striped8(idx5),
        "offs6": striped8(idx6),
    }


def reference(query, keys_words, keys_scales, notes_words, notes_scales, users_words, users_scales, offs, offs2, offs3, offs4, offs5, offs6):
    idx = unstriped8(offs)
    idx2 = unstriped8(offs2)
    idx3 = unstriped8(offs3)
    idx4 = unstriped8(offs4)
    idx5 = unstriped8(offs5)
    idx6 = unstriped8(offs6)
    keysu = unpack_weight(keys_words, keys_scales, "e2m1")
    notesu = unpack_weight(notes_words, notes_scales, "e4m3")
    usersu = unpack_weight(users_words, users_scales, "e2m1")
    queryq = mxq(f64(query), 0, "e4m3")
    a = queryq.T @ keysu
    b = queryq.T @ notesu
    c0 = queryq.T @ usersu
    w = np.minimum(pick8(a, idx, 16), pick8(b, idx2, 16))
    f1 = np.zeros((Q, X))
    f1[np.arange(Q)[:, None], idx3[np.arange(Q) % 128 // 16]] = w
    cc = np.maximum(c0, f1)
    v = pick8(cc, idx4, 16) - w
    f2 = np.zeros((Q, T))
    f2[np.arange(Q)[:, None], idx5[np.arange(Q) % 128 // 16]] = v
    aa = a + f2
    y = pick8(aa, idx6, 16)
    return y

@@ -1,0 +1,133 @@
+from contextlib import ExitStack
+
+import concourse.mybir as mybir
+
+D, POOL, SLOTS, Q = 512, 1024, 512, 128
+FLOPS = 3 * 2 * D * Q * POOL
+
+F32 = mybir.dt.float32
+BF16 = mybir.dt.bfloat16
+I32 = mybir.dt.int32
+U32 = mybir.dt.uint32
+U16 = mybir.dt.uint16
+U8 = mybir.dt.uint8
+FP8X4 = mybir.dt.float8_e4m3fn_x4
+FP4X4 = mybir.dt.float4_e2m1fn_x4
+ALU = mybir.AluOpType
+COPY = mybir.ActivationFunctionType.Copy
+
+P = 128
+PACK = 4
+BANK = 512
+HALF = SLOTS // 2
+LIST_COLS = SLOTS // 16
+
+
+def tile_attend_broker_three_kernel(tc, query, keys_words, keys_scales, notes_words, notes_scales,
+                                     users_words, users_scales, offs, offs2, offs3, offs4, offs5, offs6, out):
+    nc = tc.nc
+    with ExitStack() as ctx:
+        sb = ctx.enter_context(tc.tile_pool(name="sb", bufs=1))
+        psum = ctx.enter_context(tc.psum_pool(name="psum", bufs=1))
+
+        def load_scales(name, scales):
+            tile = sb.tile([P, POOL], U8, name=name, align_bytes=64)
+            nc.vector.memset(tile[:].bitcast(I32), 0)
+            for quad in range(4):
+                nc.sync.dma_start(out=tile[32 * quad : 32 * quad + 4, :].bitcast(I32),
+                                  in_=scales[0, 4 * quad : 4 * quad + 4, :].bitcast(I32))
+            return tile
+
+        def load_words(name, words):
+            tile = sb.tile([P, words.shape[1]], U8, name=name, align_bytes=64)
+            nc.sync.dma_start(out=tile[:].bitcast(I32), in_=words.bitcast(I32))
+            return tile
+
+        def load_list(name, lists):
+            tile = sb.tile([P, LIST_COLS], U16, name=name)
+            nc.sync.dma_start(tile[:], lists)
+            return tile
+
+        q_raw = sb.tile([P, PACK, Q], F32, name="q_raw")
+        nc.sync.dma_start(out=q_raw[:], in_=query.rearrange("(p j) q -> p j q", j=PACK))
+        keys_w = load_words("keys_w", keys_words[0])
+        keys_s = load_scales("keys_s", keys_scales)
+        notes_w = load_words("notes_w", notes_words[0].rearrange("p n t -> p (n t)"))
+        notes_s = load_scales("notes_s", notes_scales)
+        idx = load_list("idx", offs)
+        idx2 = load_list("idx2", offs2)
+        idx3 = load_list("idx3", offs3)
+        users_w = load_words("users_w", users_words[0])
+        users_s = load_scales("users_s", users_scales)
+        idx4 = load_list("idx4", offs4)
+        idx5 = load_list("idx5", offs5)
+        idx6 = load_list("idx6", offs6)
+
+        f1 = sb.tile([P, POOL], F32, name="f1")
+        f2 = sb.tile([P, POOL], F32, name="f2")
+        nc.vector.memset(f1[:], 0.0)
+        nc.vector.memset(f2[:], 0.0)
+
+        q_bf = sb.tile([P, Q, PACK], BF16, name="q_bf", align_bytes=64)
+        nc.vector.tensor_copy(out=q_bf[:].rearrange("p (c i) j -> p c j i", i=4),
+                              in_=q_raw[:].rearrange("p j (c i) -> p c j i", i=4))
+        q_codes = sb.tile([P, Q], U32, name="q_codes", align_bytes=64)
+        q_scales = sb.tile([P, Q], U8, name="q_scales", align_bytes=64)
+        nc.vector.quantize_mx(out=q_codes[:].bitcast(FP8X4), scales=q_scales[:],
+                              in_=q_bf[:].rearrange("p q j -> p (q j)"))
+
+        def score(name, words, scales, word_dtype, word_bytes):
+            banks = []
+            for h in range(POOL // BANK):
+                bank = psum.tile([P, BANK], F32, name=name + str(h))
+                nc.tensor.matmul_mx(out=bank[:], lhsT=q_codes[:].bitcast(FP8X4), lhsT_scale=q_scales[:],
+                                    rhs=words[:, h * BANK * word_bytes : (h + 1) * BANK * word_bytes].bitcast(word_dtype),
+                                    rhs_scale=scales[:, h * BANK : (h + 1) * BANK], start=True, stop=True)
+                banks.append(bank)
+            return banks
+
+        a_ps = score("a_ps", keys_w, keys_s, FP4X4, 2)
+        b_ps = score("b_ps", notes_w, notes_s, FP8X4, 4)
+        c_ps = score("c_ps", users_w, users_s, FP4X4, 2)
+
+        lo_cols, hi_cols = slice(0, BANK), slice(BANK, POOL)
+        lo, hi = slice(0, HALF), slice(HALF, SLOTS)
+        lo_list, hi_list = slice(0, LIST_COLS // 2), slice(LIST_COLS // 2, LIST_COLS)
+
+        def gather_halves(dst_lo, dst_hi, window, lists):
+            nc.vector.tensor_copy(dst_lo, window[:].indirect(lists[:, lo_list]))
+            nc.scalar.activation(dst_hi, window[:].indirect(lists[:, hi_list]), COPY)
+
+        a = sb.tile([P, POOL], F32, name="a")
+        b = sb.tile([P, POOL], F32, name="b")
+        nc.scalar.activation(a[:, lo_cols], a_ps[0][:], COPY)
+        nc.vector.tensor_copy(a[:, hi_cols], a_ps[1][:])
+        nc.scalar.activation(b[:, lo_cols], b_ps[0][:], COPY)
+        nc.scalar.activation(b[:, hi_cols], b_ps[1][:], COPY)
+
+        a_sel = sb.tile([P, SLOTS], F32, name="a_sel")
+        b_sel = sb.tile([P, SLOTS], F32, name="b_sel")
+        nc.vector.tensor_copy(a_sel[:], a[:].indirect(idx[:]))
+        gather_halves(b_sel[:, lo], b_sel[:, hi], b, idx2)
+
+        w = sb.tile([P, SLOTS], F32, name="w")
+        nc.vector.tensor_tensor(w[:], a_sel[:], b_sel[:], ALU.min)
+        nc.vector.tensor_copy(f1[:].indirect(idx3[:]), w[:])
+        w_neg = sb.tile([P, SLOTS], F32, name="w_neg")
+        nc.scalar.activation(w_neg[:], w[:], COPY, scale=-1.0)
+
+        cc = sb.tile([P, POOL], F32, name="cc")
+        nc.vector.tensor_tensor(cc[:, lo_cols], c_ps[0][:], f1[:, lo_cols], ALU.max)
+        nc.vector.tensor_tensor(cc[:, hi_cols], c_ps[1][:], f1[:, hi_cols], ALU.max)
+
+        cc_sel = sb.tile([P, SLOTS], F32, name="cc_sel")
+        gather_halves(cc_sel[:, lo], cc_sel[:, hi], cc, idx4)
+        nc.vector.tensor_tensor(f2[:].indirect(idx5[:]), cc_sel[:], w_neg[:], ALU.add)
+
+        aa = sb.tile([P, POOL], F32, name="aa")
+        nc.vector.tensor_tensor(aa[:], a[:], f2[:], ALU.add)
+
+        y = sb.tile([P, SLOTS], F32, name="y")
+        gather_halves(y[:, lo], y[:, hi], aa, idx6)
+        nc.sync.dma_start(out=out[:, lo], in_=y[:, lo])
+        nc.scalar.dma_start(out=out[:, hi], in_=y[:, hi])

@@ -30,9 +30,9 @@ def tile_attend_broker_three_kernel(tc, query, keys_words, keys_scales, notes_wo
         sb = ctx.enter_context(tc.tile_pool(name="sb", bufs=1))
         psum = ctx.enter_context(tc.psum_pool(name="psum", bufs=1))
 
-        def load_scales(name, scales):
+        def load_scales(name, scales, eng):
             tile = sb.tile([P, POOL], U8, name=name, align_bytes=64)
-            nc.vector.memset(tile[:].bitcast(I32), 0)
+            eng.memset(tile[:].bitcast(I32), 0)
             for quad in range(4):
                 nc.sync.dma_start(out=tile[32 * quad : 32 * quad + 4, :].bitcast(I32),
                                   in_=scales[0, 4 * quad : 4 * quad + 4, :].bitcast(I32))
@@ -50,15 +50,15 @@ def tile_attend_broker_three_kernel(tc, query, keys_words, keys_scales, notes_wo
 
         q_raw = sb.tile([P, PACK, Q], F32, name="q_raw")
         nc.sync.dma_start(out=q_raw[:], in_=query.rearrange("(p j) q -> p j q", j=PACK))
+        keys_s = load_scales("keys_s", keys_scales, nc.gpsimd)
         keys_w = load_words("keys_w", keys_words[0])
-        keys_s = load_scales("keys_s", keys_scales)
         notes_w = load_words("notes_w", notes_words[0].rearrange("p n t -> p (n t)"))
-        notes_s = load_scales("notes_s", notes_scales)
+        notes_s = load_scales("notes_s", notes_scales, nc.gpsimd)
         idx = load_list("idx", offs)
         idx2 = load_list("idx2", offs2)
         idx3 = load_list("idx3", offs3)
         users_w = load_words("users_w", users_words[0])
-        users_s = load_scales("users_s", users_scales)
+        users_s = load_scales("users_s", users_scales, nc.gpsimd)
         idx4 = load_list("idx4", offs4)
         idx5 = load_list("idx5", offs5)
         idx6 = load_list("idx6", offs6)
@@ -69,28 +69,38 @@ def tile_attend_broker_three_kernel(tc, query, keys_words, keys_scales, notes_wo
         nc.vector.memset(f2[:], 0.0)
 
         q_bf = sb.tile([P, Q, PACK], BF16, name="q_bf", align_bytes=64)
-        nc.vector.tensor_copy(out=q_bf[:].rearrange("p (c i) j -> p c j i", i=4),
-                              in_=q_raw[:].rearrange("p j (c i) -> p c j i", i=4))
         q_codes = sb.tile([P, Q], U32, name="q_codes", align_bytes=64)
         q_scales = sb.tile([P, Q], U8, name="q_scales", align_bytes=64)
-        nc.vector.quantize_mx(out=q_codes[:].bitcast(FP8X4), scales=q_scales[:],
-                              in_=q_bf[:].rearrange("p q j -> p (q j)"))
+        q_halves = (slice(0, Q // 2), slice(Q // 2, Q))
+        for rows in q_halves:
+            nc.vector.tensor_copy(out=q_bf[:, rows, :].rearrange("p (c i) j -> p c j i", i=4),
+                                  in_=q_raw[:, :, rows].rearrange("p j (c i) -> p c j i", i=4))
+        for rows in q_halves:
+            nc.vector.quantize_mx(out=q_codes[:, rows].bitcast(FP8X4), scales=q_scales[:, rows],
+                                  in_=q_bf[:, rows, :].rearrange("p q j -> p (q j)"))
 
-        def score(name, words, scales, word_dtype, word_bytes):
-            banks = []
-            for h in range(POOL // BANK):
-                bank = psum.tile([P, BANK], F32, name=name + str(h))
+        def score(tags, widths, words, scales, word_dtype, word_bytes):
+            pieces, first = [], 0
+            for tag, width in zip(tags, widths):
+                cols = slice(first, first + width)
+                bank = psum.tile([P, width], F32, name=tag)
                 nc.tensor.matmul_mx(out=bank[:], lhsT=q_codes[:].bitcast(FP8X4), lhsT_scale=q_scales[:],
-                                    rhs=words[:, h * BANK * word_bytes : (h + 1) * BANK * word_bytes].bitcast(word_dtype),
-                                    rhs_scale=scales[:, h * BANK : (h + 1) * BANK], start=True, stop=True)
-                banks.append(bank)
-            return banks
+                                    rhs=words[:, cols.start * word_bytes : cols.stop * word_bytes].bitcast(word_dtype),
+                                    rhs_scale=scales[:, cols], start=True, stop=True)
+                pieces.append((cols, bank))
+                first = cols.stop
+            return pieces
 
-        a_ps = score("a_ps", keys_w, keys_s, FP4X4, 2)
-        b_ps = score("b_ps", notes_w, notes_s, FP8X4, 4)
-        c_ps = score("c_ps", users_w, users_s, FP4X4, 2)
+        a_ps = score(["a0", "a1", "a2", "a3"], [256,256,256,256], keys_w, keys_s, FP4X4, 2)
+        b_ps = score(["b0", "b1", "b2", "b3"], [256,256,256,256], notes_w, notes_s, FP8X4, 4)
 
-        lo_cols, hi_cols = slice(0, BANK), slice(BANK, POOL)
+        def evacuate(dst, piece, on_scalar):
+            cols, bank = piece
+            if on_scalar:
+                nc.scalar.activation(dst[:, cols], bank[:], COPY)
+            else:
+                nc.vector.tensor_copy(dst[:, cols], bank[:])
+
         lo, hi = slice(0, HALF), slice(HALF, SLOTS)
         lo_list, hi_list = slice(0, LIST_COLS // 2), slice(LIST_COLS // 2, LIST_COLS)
 
@@ -100,25 +110,27 @@ def tile_attend_broker_three_kernel(tc, query, keys_words, keys_scales, notes_wo
 
         a = sb.tile([P, POOL], F32, name="a")
         b = sb.tile([P, POOL], F32, name="b")
-        nc.scalar.activation(a[:, lo_cols], a_ps[0][:], COPY)
-        nc.vector.tensor_copy(a[:, hi_cols], a_ps[1][:])
-        nc.scalar.activation(b[:, lo_cols], b_ps[0][:], COPY)
-        nc.scalar.activation(b[:, hi_cols], b_ps[1][:], COPY)
-
         a_sel = sb.tile([P, SLOTS], F32, name="a_sel")
         b_sel = sb.tile([P, SLOTS], F32, name="b_sel")
-        nc.vector.tensor_copy(a_sel[:], a[:].indirect(idx[:]))
+        for piece, on_scalar in zip(a_ps, (True, False, True, False)):
+            evacuate(a, piece, on_scalar)
+        nc.vector.tensor_copy(a_sel[:, lo], a[:].indirect(idx[:, lo_list]))
+        for piece, on_scalar in zip(b_ps, (True, True, True, False)):
+            evacuate(b, piece, on_scalar)
+        nc.scalar.activation(a_sel[:, hi], a[:].indirect(idx[:, hi_list]), COPY)
         gather_halves(b_sel[:, lo], b_sel[:, hi], b, idx2)
+        c_ps = score(["b0", "b1"], [BANK, BANK], users_w, users_s, FP4X4, 2)
 
         w = sb.tile([P, SLOTS], F32, name="w")
-        nc.vector.tensor_tensor(w[:], a_sel[:], b_sel[:], ALU.min)
+        for slots in (lo, hi):
+            nc.vector.tensor_tensor(w[:, slots], a_sel[:, slots], b_sel[:, slots], ALU.min)
         nc.vector.tensor_copy(f1[:].indirect(idx3[:]), w[:])
         w_neg = sb.tile([P, SLOTS], F32, name="w_neg")
         nc.scalar.activation(w_neg[:], w[:], COPY, scale=-1.0)
 
         cc = sb.tile([P, POOL], F32, name="cc")
-        nc.vector.tensor_tensor(cc[:, lo_cols], c_ps[0][:], f1[:, lo_cols], ALU.max)
-        nc.vector.tensor_tensor(cc[:, hi_cols], c_ps[1][:], f1[:, hi_cols], ALU.max)
+        for cols, bank in c_ps:
+            nc.vector.tensor_tensor(cc[:, cols], bank[:], f1[:, cols], ALU.max)
 
         cc_sel = sb.tile([P, SLOTS], F32, name="cc_sel")
         gather_halves(cc_sel[:, lo], cc_sel[:, hi], cc, idx4)

@@ -30,9 +30,8 @@ def tile_attend_broker_three_kernel(tc, query, keys_words, keys_scales, notes_wo
         sb = ctx.enter_context(tc.tile_pool(name="sb", bufs=1))
         psum = ctx.enter_context(tc.psum_pool(name="psum", bufs=1))
 
-        def load_scales(name, scales, eng):
+        def load_scales(name, scales):
             tile = sb.tile([P, POOL], U8, name=name, align_bytes=64)
-            eng.memset(tile[:].bitcast(I32), 0)
             for quad in range(4):
                 nc.sync.dma_start(out=tile[32 * quad : 32 * quad + 4, :].bitcast(I32),
                                   in_=scales[0, 4 * quad : 4 * quad + 4, :].bitcast(I32))
@@ -50,15 +49,15 @@ def tile_attend_broker_three_kernel(tc, query, keys_words, keys_scales, notes_wo
 
         q_raw = sb.tile([P, PACK, Q], F32, name="q_raw")
         nc.sync.dma_start(out=q_raw[:], in_=query.rearrange("(p j) q -> p j q", j=PACK))
-        keys_s = load_scales("keys_s", keys_scales, nc.gpsimd)
+        keys_s = load_scales("keys_s", keys_scales)
         keys_w = load_words("keys_w", keys_words[0])
         notes_w = load_words("notes_w", notes_words[0].rearrange("p n t -> p (n t)"))
-        notes_s = load_scales("notes_s", notes_scales, nc.gpsimd)
+        notes_s = load_scales("notes_s", notes_scales)
         idx = load_list("idx", offs)
         idx2 = load_list("idx2", offs2)
         idx3 = load_list("idx3", offs3)
         users_w = load_words("users_w", users_words[0])
-        users_s = load_scales("users_s", users_scales, nc.gpsimd)
+        users_s = load_scales("users_s", users_scales)
         idx4 = load_list("idx4", offs4)
         idx5 = load_list("idx5", offs5)
         idx6 = load_list("idx6", offs6)

from contextlib import ExitStack

import concourse.mybir as mybir

D, POOL, SLOTS, Q = 512, 1024, 512, 128
FLOPS = 3 * 2 * D * Q * POOL

F32 = mybir.dt.float32
BF16 = mybir.dt.bfloat16
I32 = mybir.dt.int32
U32 = mybir.dt.uint32
U16 = mybir.dt.uint16
U8 = mybir.dt.uint8
FP8X4 = mybir.dt.float8_e4m3fn_x4
FP4X4 = mybir.dt.float4_e2m1fn_x4
ALU = mybir.AluOpType
COPY = mybir.ActivationFunctionType.Copy

P = 128
PACK = 4
BANK = 512
HALF = SLOTS // 2
LIST_COLS = SLOTS // 16


def tile_attend_broker_three_kernel(tc, query, keys_words, keys_scales, notes_words, notes_scales,
                                     users_words, users_scales, offs, offs2, offs3, offs4, offs5, offs6, out):
    nc = tc.nc
    with ExitStack() as ctx:
        sb = ctx.enter_context(tc.tile_pool(name="sb", bufs=1))
        psum = ctx.enter_context(tc.psum_pool(name="psum", bufs=1))

        def load_scales(name, scales):
            tile = sb.tile([P, POOL], U8, name=name, align_bytes=64)
            for quad in range(4):
                nc.sync.dma_start(out=tile[32 * quad : 32 * quad + 4, :].bitcast(I32),
                                  in_=scales[0, 4 * quad : 4 * quad + 4, :].bitcast(I32))
            return tile

        def load_words(name, words):
            tile = sb.tile([P, words.shape[1]], U8, name=name, align_bytes=64)
            nc.sync.dma_start(out=tile[:].bitcast(I32), in_=words.bitcast(I32))
            return tile

        def load_list(name, lists):
            tile = sb.tile([P, LIST_COLS], U16, name=name)
            nc.sync.dma_start(tile[:], lists)
            return tile

        q_raw = sb.tile([P, PACK, Q], F32, name="q_raw")
        nc.sync.dma_start(out=q_raw[:], in_=query.rearrange("(p j) q -> p j q", j=PACK))
        keys_s = load_scales("keys_s", keys_scales)
        keys_w = load_words("keys_w", keys_words[0])
        notes_w = load_words("notes_w", notes_words[0].rearrange("p n t -> p (n t)"))
        notes_s = load_scales("notes_s", notes_scales)
        idx = load_list("idx", offs)
        idx2 = load_list("idx2", offs2)
        idx3 = load_list("idx3", offs3)
        users_w = load_words("users_w", users_words[0])
        users_s = load_scales("users_s", users_scales)
        idx4 = load_list("idx4", offs4)
        idx5 = load_list("idx5", offs5)
        idx6 = load_list("idx6", offs6)

        f1 = sb.tile([P, POOL], F32, name="f1")
        f2 = sb.tile([P, POOL], F32, name="f2")
        nc.vector.memset(f1[:], 0.0)
        nc.vector.memset(f2[:], 0.0)

        q_bf = sb.tile([P, Q, PACK], BF16, name="q_bf", align_bytes=64)
        q_codes = sb.tile([P, Q], U32, name="q_codes", align_bytes=64)
        q_scales = sb.tile([P, Q], U8, name="q_scales", align_bytes=64)
        q_halves = (slice(0, Q // 2), slice(Q // 2, Q))
        for rows in q_halves:
            nc.vector.tensor_copy(out=q_bf[:, rows, :].rearrange("p (c i) j -> p c j i", i=4),
                                  in_=q_raw[:, :, rows].rearrange("p j (c i) -> p c j i", i=4))
        for rows in q_halves:
            nc.vector.quantize_mx(out=q_codes[:, rows].bitcast(FP8X4), scales=q_scales[:, rows],
                                  in_=q_bf[:, rows, :].rearrange("p q j -> p (q j)"))

        def score(tags, widths, words, scales, word_dtype, word_bytes):
            pieces, first = [], 0
            for tag, width in zip(tags, widths):
                cols = slice(first, first + width)
                bank = psum.tile([P, width], F32, name=tag)
                nc.tensor.matmul_mx(out=bank[:], lhsT=q_codes[:].bitcast(FP8X4), lhsT_scale=q_scales[:],
                                    rhs=words[:, cols.start * word_bytes : cols.stop * word_bytes].bitcast(word_dtype),
                                    rhs_scale=scales[:, cols], start=True, stop=True)
                pieces.append((cols, bank))
                first = cols.stop
            return pieces

        a_ps = score(["a0", "a1", "a2", "a3"], [256,256,256,256], keys_w, keys_s, FP4X4, 2)
        b_ps = score(["b0", "b1", "b2", "b3"], [256,256,256,256], notes_w, notes_s, FP8X4, 4)

        def evacuate(dst, piece, on_scalar):
            cols, bank = piece
            if on_scalar:
                nc.scalar.activation(dst[:, cols], bank[:], COPY)
            else:
                nc.vector.tensor_copy(dst[:, cols], bank[:])

        lo, hi = slice(0, HALF), slice(HALF, SLOTS)
        lo_list, hi_list = slice(0, LIST_COLS // 2), slice(LIST_COLS // 2, LIST_COLS)

        def gather_halves(dst_lo, dst_hi, window, lists):
            nc.vector.tensor_copy(dst_lo, window[:].indirect(lists[:, lo_list]))
            nc.scalar.activation(dst_hi, window[:].indirect(lists[:, hi_list]), COPY)

        a = sb.tile([P, POOL], F32, name="a")
        b = sb.tile([P, POOL], F32, name="b")
        a_sel = sb.tile([P, SLOTS], F32, name="a_sel")
        b_sel = sb.tile([P, SLOTS], F32, name="b_sel")
        for piece, on_scalar in zip(a_ps, (True, False, True, False)):
            evacuate(a, piece, on_scalar)
        nc.vector.tensor_copy(a_sel[:, lo], a[:].indirect(idx[:, lo_list]))
        for piece, on_scalar in zip(b_ps, (True, True, True, False)):
            evacuate(b, piece, on_scalar)
        nc.scalar.activation(a_sel[:, hi], a[:].indirect(idx[:, hi_list]), COPY)
        gather_halves(b_sel[:, lo], b_sel[:, hi], b, idx2)
        c_ps = score(["b0", "b1"], [BANK, BANK], users_w, users_s, FP4X4, 2)

        w = sb.tile([P, SLOTS], F32, name="w")
        for slots in (lo, hi):
            nc.vector.tensor_tensor(w[:, slots], a_sel[:, slots], b_sel[:, slots], ALU.min)
        nc.vector.tensor_copy(f1[:].indirect(idx3[:]), w[:])
        w_neg = sb.tile([P, SLOTS], F32, name="w_neg")
        nc.scalar.activation(w_neg[:], w[:], COPY, scale=-1.0)

        cc = sb.tile([P, POOL], F32, name="cc")
        for cols, bank in c_ps:
            nc.vector.tensor_tensor(cc[:, cols], bank[:], f1[:, cols], ALU.max)

        cc_sel = sb.tile([P, SLOTS], F32, name="cc_sel")
        gather_halves(cc_sel[:, lo], cc_sel[:, hi], cc, idx4)
        nc.vector.tensor_tensor(f2[:].indirect(idx5[:]), cc_sel[:], w_neg[:], ALU.add)

        aa = sb.tile([P, POOL], F32, name="aa")
        nc.vector.tensor_tensor(aa[:], a[:], f2[:], ALU.add)

        y = sb.tile([P, SLOTS], F32, name="y")
        gather_halves(y[:, lo], y[:, hi], aa, idx6)
        nc.sync.dma_start(out=out[:, lo], in_=y[:, lo])
        nc.scalar.dma_start(out=out[:, hi], in_=y[:, hi])
